import numpy as np
import ml_dtypes


def mxq(x, axis, fmt="e4m3"):
    dtype, down = {"e4m3": (ml_dtypes.float8_e4m3fn, 7), "e5m2": (ml_dtypes.float8_e5m2, 14)}[fmt]
    v = np.moveaxis(np.asarray(x, np.float32).astype(ml_dtypes.bfloat16).astype(np.float64), axis, -1)
    blocks = v.reshape(v.shape[:-1] + (-1, 32))
    amax = np.abs(blocks).max(-1, keepdims=True)
    byte = np.maximum(np.where(amax > 0, np.frexp(amax)[1] - 1 + 127, 0) - down, 1)
    scale = np.exp2(byte - 127.0)
    codes = (blocks / scale).astype(np.float32).astype(dtype).astype(np.float64)
    return np.moveaxis((codes * scale).reshape(v.shape), -1, axis)


WIDE = False


def mx_kscale(k):
    if not WIDE:
        return np.ones(k)
    levels = np.array([10, -10, 5, -5, 0])
    if k % 512:
        return np.exp2(np.random.permutation(np.resize(levels, k // 32))).repeat(32)
    a = np.empty((k // 512, 16))
    for p in range(k // 512):
        a[p, :8] = np.random.permutation(np.resize(levels, 8))
        for g in range(8):
            far = levels[np.abs(levels - a[p, g]) >= 10]
            a[p, g + 8] = far[np.random.randint(len(far))]
    return np.exp2(a.ravel()).repeat(32)


BF16 = ml_dtypes.bfloat16


def bf(x):
    return np.asarray(x, np.float32).astype(BF16)


def f64(x):
    return np.asarray(x).astype(np.float64)

def planes(Y):
    n, m = Y.shape
    b = f64(bf(Y)).reshape(n // 32, 32, m)
    amax = np.abs(b).max(1)
    byte = np.clip(np.where(amax > 0, np.frexp(amax)[1] - 1 + 127 - 7, 1), 1, 254)
    codes = (b * np.exp2(127.0 - byte)[:, None, :]).reshape(n, m).astype(np.float32).astype(ml_dtypes.float8_e4m3fn).view(np.uint8)
    words = codes.reshape(n // 512, 128, 4, m).transpose(0, 1, 3, 2)
    return np.ascontiguousarray(words), np.ascontiguousarray(byte.astype(np.uint8).reshape(n // 512, 16, m))


TOKENS, MODEL, HIDDEN = 2048, 1536, 1024

GAIN_SPREAD = 0.8
TEMP_SPREAD = 0.3
BIAS_SIZE = 0.4


def setup_inputs():
    s = mx_kscale(MODEL)
    x = np.random.randn(TOKENS, MODEL) * s[None, :]
    w_hidden = np.random.randn(MODEL, HIDDEN) / np.sqrt(MODEL) / s[:, None]
    b_hidden = BIAS_SIZE * np.random.randn(HIDDEN)
    gain = np.exp(GAIN_SPREAD * np.random.randn(HIDDEN))
    inv_temp = np.exp(TEMP_SPREAD * np.random.randn(TOKENS))
    return {"x": bf(x), "w_hidden": bf(w_hidden), "b_hidden": bf(b_hidden),
            "gain": bf(gain), "inv_temp": bf(inv_temp)}


def reference(x, w_hidden, b_hidden, gain, inv_temp):
    xq = mxq(f64(x), 1, "e4m3")
    wq = mxq(f64(w_hidden), 0, "e4m3")
    pre = xq @ wq
    hidden = np.tanh(pre + f64(b_hidden)[None, :])
    y = hidden * f64(gain)[None, :] * f64(inv_temp)[:, None]
    Y = y.T
    words, scales = planes(Y)
    return y, words, scales

@@ -1,0 +1,324 @@
+from contextlib import ExitStack
+
+import concourse.mybir as mybir
+from concourse.masks import make_identity
+
+TOKENS, MODEL, HIDDEN = 2048, 1536, 1024
+FLOPS = 2 * TOKENS * MODEL * HIDDEN
+
+F32 = mybir.dt.float32
+BF16 = mybir.dt.bfloat16
+U32 = mybir.dt.uint32
+I32 = mybir.dt.int32
+U8 = mybir.dt.uint8
+FP8X4 = mybir.dt.float8_e4m3fn_x4
+TANH = mybir.ActivationFunctionType.Tanh
+MULT = mybir.AluOpType.mult
+
+P = 128
+PACK = 4
+K_PASS = P * PACK
+PASSES = MODEL // K_PASS
+GROUPS = HIDDEN // K_PASS
+BLOCK = 512
+BLOCKS = TOKENS // BLOCK
+BANKS = 8
+SPLIT_LOAD_BLOCKS = 2
+LAST_PIECES = (256, 256)
+HEAD_X = ("vector", "scalar", "vector", "vector", "scalar", "scalar")
+PLAN_X = "g0 w0 z0 m0 m1 s0 s1 x0 x1 x2 w1 q0 x3 q1 m2 m3 s2 v0 s3 x4 x5 q2 y0 y1 y2 y3"
+PLAN_W = "g0 w0 z0 m0 m1 w1 s0 v0 s1 m2 m3 s2 s3 y0 y1 y2 y3"
+PLAN_Y = "g0 m0 m1 s0 z0 s1 m2 m3 s2 s3 y0 y1 y2 y3"
+PLAN_T = "g0 m0 m1 s0 z0 s1 m2 m3 s2 s3 y0 y1 y2 y3"
+
+
+def tile_router_hidden_tanh_g1_kernel(tc, x, w_hidden, b_hidden, gain, inv_temp, out_0, out_1, out_2):
+    nc = tc.nc
+    words_out = out_1.rearrange("g p m t -> g p (m t)").bitcast(I32)
+    scales_out = out_2.bitcast(I32)
+
+    with ExitStack() as ctx:
+        keep = ctx.enter_context(tc.tile_pool(name="keep", bufs=1))
+        work = ctx.enter_context(tc.tile_pool(name="work", bufs=2))
+        psum = ctx.enter_context(tc.psum_pool(name="psum", bufs=1))
+        ctx.enter_context(tc.manual_schedule())
+
+        bank_queue = list(range(BANKS))
+
+        def take_bank():
+            number = bank_queue[0]
+            bank_queue.remove(number)
+            bank = psum.tile([P, BLOCK], F32, name="bank%d" % number)
+            return number, bank
+
+        def copy_on(engine, out, in_):
+            if engine == "scalar":
+                nc.scalar.copy(out=out, in_=in_)
+            else:
+                nc.vector.tensor_copy(out=out, in_=in_)
+
+        temp_rows = keep.tile([P, TOKENS // P], BF16)
+        bias = keep.tile([P, GROUPS, PACK], BF16)
+        gains = keep.tile([P, GROUPS, PACK], BF16)
+        nc.scalar.dma_start(out=temp_rows[:], in_=inv_temp.rearrange("(n j) -> n j", n=P))
+        nc.scalar.dma_start(out=bias[:], in_=b_hidden.rearrange("(g p t) -> p g t", p=P, t=PACK))
+        nc.scalar.dma_start(out=gains[:], in_=gain.rearrange("(g p t) -> p g t", p=P, t=PACK))
+
+        ident = keep.tile([P, P], F32)
+        make_identity(nc, ident[:])
+        warm = keep.tile([P, 2], F32)
+        nc.vector.memset(warm[:, 0:1], 0.0)
+        nc.scalar.activation(out=warm[:, 1:2], in_=warm[:, 0:1], func=TANH)
+
+        x_words = {}
+        w_raw = {}
+
+        def load_x_pass(b, c):
+            raw = keep.tile([P, BLOCK // P, K_PASS], BF16, name="x_raw%d_%d" % (b, c))
+            rows = x[b * BLOCK : (b + 1) * BLOCK, c * K_PASS : (c + 1) * K_PASS]
+            nc.sync.dma_start(out=raw[:], in_=rows.rearrange("(j p) k -> p j k", p=P))
+            x_words[b, c] = raw[:].bitcast(F32)
+
+        def load_x_block(b):
+            raw = keep.tile([P, BLOCK // P, MODEL], BF16, name="x_raw%d" % b)
+            rows = x[b * BLOCK : (b + 1) * BLOCK, :]
+            nc.sync.dma_start(out=raw[:], in_=rows.rearrange("(j p) k -> p j k", p=P))
+            for c in range(PASSES):
+                x_words[b, c] = raw[:, :, c * K_PASS : (c + 1) * K_PASS].bitcast(F32)
+
+        def load_w(g, c):
+            raw = keep.tile([P, PACK, K_PASS], BF16, name="w_raw%d_%d" % (g, c))
+            rows = w_hidden[c * K_PASS : (c + 1) * K_PASS, g * K_PASS : (g + 1) * K_PASS]
+            nc.sync.dma_start(out=raw[:], in_=rows.rearrange("(p j) n -> p j n", j=PACK))
+            w_raw[g, c] = raw
+
+        for c in range(PASSES):
+            load_x_pass(0, c)
+            load_w(0, c)
+        for c in range(PASSES):
+            load_x_pass(1, c)
+        load_w(1, 0)
+        load_x_block(2)
+        load_w(1, 1)
+        load_w(1, 2)
+        load_x_block(3)
+
+        temp_all = keep.tile([P, TOKENS], BF16)
+        temp_pairs = temp_rows[:].bitcast(F32)
+        temp_all_pairs = temp_all[:].bitcast(F32).rearrange("p (n w) -> p n w", n=P)
+        for half in range(2):
+            number, bank = take_bank()
+            for w in range(PACK):
+                column = temp_pairs[:, PACK * half + w : PACK * half + w + 1]
+                nc.tensor.transpose(bank[:, w * P : (w + 1) * P], column.to_broadcast([P, P]), ident[:])
+            bank_queue.append(number)
+            nc.scalar.copy(
+                out=temp_all_pairs[:, :, PACK * half : PACK * (half + 1)],
+                in_=bank[:].rearrange("p (w n) -> p n w", w=PACK),
+            )
+
+        x_codes = [keep.tile([P, PASSES, BLOCK], U32, name="x_codes%d" % b, align_bytes=64) for b in range(BLOCKS)]
+        x_scales = [keep.tile([P, PASSES, BLOCK], U8, name="x_scales%d" % b, align_bytes=64) for b in range(BLOCKS)]
+        w_codes = [keep.tile([P, PASSES, K_PASS], U32, name="w_codes%d" % g, align_bytes=64) for g in range(GROUPS)]
+        w_scales = [keep.tile([P, PASSES, K_PASS], U8, name="w_scales%d" % g, align_bytes=64) for g in range(GROUPS)]
+        y_scales = [keep.tile([P, TOKENS], U8, name="y_scales%d" % g, align_bytes=64) for g in range(GROUPS)]
+        x_grouped = {}
+        w_grouped = {}
+        hidden = {}
+        y_turned = {}
+        y_grouped = {}
+
+        def turn_x(b, c, half, engine):
+            if half == 0:
+                x_grouped[b, c] = work.tile([P, BLOCK * PACK], BF16, name="x_grouped", bufs=3, align_bytes=64)
+            number, bank = take_bank()
+            for jj in range(2):
+                for u in range(2):
+                    columns = slice(2 * P * u + P * jj, 2 * P * u + P * (jj + 1))
+                    nc.tensor.transpose(bank[:, columns], x_words[b, c][:, 2 * half + jj, u : 2 * P : 2], ident[:])
+            bank_queue.append(number)
+            target = x_grouped[b, c][:].bitcast(F32)[:, BLOCK * half : BLOCK * (half + 1)]
+            copy_on(engine, target.rearrange("p (n u) -> p n u", u=2), bank[:].rearrange("p (u n) -> p n u", u=2))
+
+        def quantize_x(b, c):
+            nc.vector.quantize_mx(
+                out=x_codes[b][:, c, :].bitcast(FP8X4), scales=x_scales[b][:, c, :], in_=x_grouped[b, c][:]
+            )
+
+        def group_w(g, c, half, engine):
+            if half == 0:
+                w_grouped[g, c] = work.tile([P, K_PASS * PACK], BF16, name="w_grouped", bufs=3, align_bytes=64)
+            target = w_grouped[g, c][:].rearrange("p (t m j) -> p t m j", t=PACK, j=PACK)
+            source = w_raw[g, c][:].rearrange("p j (m t) -> p t m j", t=PACK)
+            copy_on(engine, target[:, 2 * half : 2 * half + 2], source[:, 2 * half : 2 * half + 2])
+
+        def quantize_w(g, c):
+            nc.vector.quantize_mx(
+                out=w_codes[g][:, c, :].bitcast(FP8X4), scales=w_scales[g][:, c, :], in_=w_grouped[g, c][:]
+            )
+
+        def mx_pass(unit, t, c, bank):
+            g, first, count = unit
+            b, start = divmod(first, BLOCK)
+            channels = slice(t * P, (t + 1) * P)
+            tokens = slice(start, start + count)
+            nc.tensor.matmul_mx(
+                out=bank[:, 0:count],
+                lhsT=w_codes[g][:, c, channels].bitcast(FP8X4),
+                lhsT_scale=w_scales[g][:, c, channels],
+                rhs=x_codes[b][:, c, tokens].bitcast(FP8X4),
+                rhs_scale=x_scales[b][:, c, tokens],
+                start=(c == 0),
+                stop=(c == PASSES - 1),
+            )
+
+        def activate(unit, t, bank):
+            g, first, count = unit
+            hidden[unit, t] = work.tile([P, BLOCK], F32, name="hidden", bufs=4)
+            nc.scalar.activation(
+                out=hidden[unit, t][:, 0:count], in_=bank[:, 0:count], func=TANH, bias=bias[:, g, t : t + 1]
+            )
+
+        def multiply(unit, t):
+            number, bank = take_bank()
+            for c in range(PASSES):
+                mx_pass(unit, t, c, bank)
+            bank_queue.append(number)
+            activate(unit, t, bank)
+
+        def scale_y(unit, t):
+            g, first, count = unit
+            if t == 0:
+                y_turned[unit] = work.tile([P, PACK, BLOCK], F32, name="y_turned", bufs=3)
+            nc.vector.scalar_tensor_tensor(
+                out=y_turned[unit][:, t, 0:count],
+                in0=temp_all[:, first : first + count],
+                scalar=gains[:, g, t : t + 1],
+                in1=hidden[unit, t][:, 0:count],
+                op0=MULT,
+                op1=MULT,
+            )
+
+        def group_y(unit):
+            g, first, count = unit
+            y_grouped[unit] = work.tile([P, BLOCK * PACK], BF16, name="y_grouped", bufs=2, align_bytes=64)
+            nc.vector.tensor_copy(
+                out=y_grouped[unit][:, 0 : count * PACK].rearrange("p (n t) -> p n t", t=PACK),
+                in_=y_turned[unit][:, :, 0:count].rearrange("p t n -> p n t"),
+            )
+
+        def quantize_y(unit):
+            g, first, count = unit
+            y_codes = work.tile([P, BLOCK], U32, name="y_codes", bufs=3, align_bytes=64)
+            nc.vector.quantize_mx(
+                out=y_codes[:, 0:count].bitcast(FP8X4),
+                scales=y_scales[g][:, first : first + count],
+                in_=y_grouped[unit][:, 0 : count * PACK],
+            )
+            nc.sync.dma_start(out=words_out[g, :, first : first + count], in_=y_codes[:, 0:count].bitcast(I32))
+
+        def store_scales(g, first, count):
+            columns = slice(first // 4, (first + count) // 4)
+            for q in range(4):
+                nc.sync.dma_start(
+                    out=scales_out[g, 4 * q : 4 * q + 4, columns],
+                    in_=y_scales[g][32 * q : 32 * q + 4, :].bitcast(I32)[:, columns],
+                )
+
+        def turn_y(unit, j, engine):
+            g, first, count = unit
+            number, bank = take_bank()
+            for t in range(PACK):
+                nc.tensor.transpose(bank[:, t * P : (t + 1) * P], y_turned[unit][:, t, j * P : (j + 1) * P], ident[:])
+            bank_queue.append(number)
+            y_rows = work.tile([P, K_PASS], F32, name="y_rows", bufs=6)
+            copy_on(
+                engine,
+                y_rows[:].rearrange("p (m t) -> p m t", t=PACK),
+                bank[:].rearrange("p (t m) -> p m t", t=PACK),
+            )
+            row = first + j * P
+            nc.sync.dma_start(out=out_0[row : row + P, g * K_PASS : (g + 1) * K_PASS], in_=y_rows[:])
+
+        units = [(g, b * BLOCK, BLOCK) for g in range(GROUPS) for b in range(BLOCKS)][:-1]
+        first = TOKENS - BLOCK
+        for count in LAST_PIECES:
+            units.append((GROUPS - 1, first, count))
+            first += count
+
+        head = units[0]
+        open_banks = []
+        for c in range(PASSES):
+            turn_x(0, c, 0, "scalar")
+            turn_x(0, c, 1, "scalar")
+            if c > 0:
+                for t in range(PACK):
+                    if c == 1:
+                        open_banks.append(take_bank())
+                    mx_pass(head, t, c - 1, open_banks[t][1])
+            group_w(0, c, 0, "vector")
+            group_w(0, c, 1, "scalar")
+            quantize_x(0, c)
+            quantize_w(0, c)
+        turn_x(1, 0, 0, HEAD_X[0])
+        turn_x(1, 0, 1, HEAD_X[1])
+        for t in range(PACK):
+            mx_pass(head, t, PASSES - 1, open_banks[t][1])
+            bank_queue.append(open_banks[t][0])
+            activate(head, t, open_banks[t][1])
+        quantize_x(1, 0)
+        turn_x(1, 1, 0, HEAD_X[2])
+        turn_x(1, 1, 1, HEAD_X[3])
+        scale_y(head, 0)
+        quantize_x(1, 1)
+        turn_x(1, 2, 0, HEAD_X[4])
+        turn_x(1, 2, 1, HEAD_X[5])
+        scale_y(head, 1)
+        quantize_x(1, 2)
+        scale_y(head, 2)
+        scale_y(head, 3)
+
+        for i in range(1, len(units)):
+            unit, before = units[i], units[i - 1]
+            tiles = before[2] // P
+            if i < BLOCKS - 1:
+                steps = PLAN_X
+            elif i == BLOCKS - 1:
+                steps = PLAN_W
+            elif unit[2] == BLOCK:
+                steps = PLAN_Y
+            else:
+                steps = PLAN_T
+            for step in steps.split():
+                kind, n = step[0], int(step[1])
+                engine = "vector" if len(step) > 2 else "scalar"
+                if kind == "m":
+                    multiply(unit, n)
+                elif kind == "s":
+                    scale_y(unit, n)
+                elif kind == "x":
+                    turn_x(i + 1, n // 2, n % 2, engine)
+                elif kind == "q":
+                    quantize_x(i + 1, n)
+                elif kind == "y":
+                    if n < tiles:
+                        turn_y(before, n, engine)
+                elif kind == "g":
+                    group_y(before)
+                elif kind == "z":
+                    quantize_y(before)
+                    if before[1] + before[2] == TOKENS:
+                        store_scales(before[0], 0, TOKENS)
+                    if i == len(units) - 1:
+                        store_scales(unit[0], 0, unit[1])
+                elif kind == "w":
+                    group_w(1, i - 1, n, "vector")
+                elif kind == "v":
+                    quantize_w(1, i - 1)
+
+        last = units[-1]
+        group_y(last)
+        for j in range(last[2] // P):
+            turn_y(last, j, "scalar")
+        quantize_y(last)
+        store_scales(last[0], last[1], last[2])

@@ -23,13 +23,215 @@ GROUPS = HIDDEN // K_PASS
 BLOCK = 512
 BLOCKS = TOKENS // BLOCK
 BANKS = 8
-SPLIT_LOAD_BLOCKS = 2
-LAST_PIECES = (256, 256)
-HEAD_X = ("vector", "scalar", "vector", "vector", "scalar", "scalar")
-PLAN_X = "g0 w0 z0 m0 m1 s0 s1 x0 x1 x2 w1 q0 x3 q1 m2 m3 s2 v0 s3 x4 x5 q2 y0 y1 y2 y3"
-PLAN_W = "g0 w0 z0 m0 m1 w1 s0 v0 s1 m2 m3 s2 s3 y0 y1 y2 y3"
-PLAN_Y = "g0 m0 m1 s0 z0 s1 m2 m3 s2 s3 y0 y1 y2 y3"
-PLAN_T = "g0 m0 m1 s0 z0 s1 m2 m3 s2 s3 y0 y1 y2 y3"
+LOADS = ((0, 2, 0, 1), (0, 0), (0, 2, 1, 1), (0, 1), (0, 2, 2, 1), (0, 2), (2, 2, 0, 1), (2, 2, 1, 1), (2, 2, 2, 1), (4, 2, 0, 3), (1, 0), (6, 2, 0, 3), (1, 1), (1, 2))
+UNITS = ((0, 0, 512), (0, 512, 512), (0, 1024, 512), (0, 1536, 512), (1, 0, 512), (1, 512, 512), (1, 1024, 512), (1, 1536, 256), (1, 1792, 256))
+PLAN = (
+    ("x", 0, 0, 1, 0),
+    ("w", 0, 0, 1, 0),
+    ("w", 0, 0, 0, 1),
+    ("x", 0, 0, 0, 0),
+    ("w", 0, 1, 1, 0),
+    ("v", 0, 0),
+    ("w", 0, 1, 0, 0),
+    ("q", 0, 0, 0, 512),
+    ("x", 0, 1, 0, 1),
+    ("x", 0, 1, 1, 1),
+    ("q", 0, 1, 0, 512),
+    ("v", 0, 1),
+    ("w", 0, 2, 0, 1),
+    ("p", 0, 0, 0),
+    ("p", 0, 1, 0),
+    ("p", 0, 2, 0),
+    ("p", 0, 3, 0),
+    ("w", 0, 2, 1, 0),
+    ("x", 0, 2, 1, 0),
+    ("x", 0, 2, 0, 1),
+    ("p", 0, 0, 1),
+    ("p", 0, 1, 1),
+    ("p", 0, 2, 1),
+    ("p", 0, 3, 1),
+    ("q", 0, 2, 0, 512),
+    ("x", 1, 0, 0, 0),
+    ("v", 0, 2),
+    ("x", 1, 0, 1, 1),
+    ("p", 0, 1, 2),
+    ("p", 0, 0, 2),
+    ("q", 1, 0, 0, 512),
+    ("s", 0, 0),
+    ("x", 1, 2, 1, 0),
+    ("p", 0, 3, 2),
+    ("s", 0, 1),
+    ("x", 1, 1, 0, 0),
+    ("x", 1, 1, 1, 1),
+    ("p", 0, 2, 2),
+    ("s", 0, 3),
+    ("x", 1, 2, 0, 0),
+    ("q", 1, 1, 0, 512),
+    ("q", 1, 2, 0, 512),
+    ("s", 0, 2),
+    ("x", 2, 0, 0, 0),
+    ("m", 1, 1),
+    ("w", 1, 0, 0, 1),
+    ("g", 0, 0),
+    ("m", 1, 0),
+    ("x", 2, 1, 0, 0),
+    ("g", 0, 1),
+    ("s", 1, 0),
+    ("z", 0),
+    ("y", 0, 0, 0),
+    ("c", 0),
+    ("s", 1, 1),
+    ("y", 0, 1, 0),
+    ("x", 2, 1, 1, 0),
+    ("x", 2, 0, 1, 0),
+    ("x", 2, 2, 1, 0),
+    ("m", 1, 3),
+    ("w", 1, 0, 1, 1),
+    ("m", 1, 2),
+    ("q", 2, 1, 0, 512),
+    ("x", 2, 2, 0, 0),
+    ("q", 2, 0, 0, 512),
+    ("s", 1, 3),
+    ("s", 1, 2),
+    ("q", 2, 2, 0, 512),
+    ("y", 0, 3, 0),
+    ("y", 0, 2, 0),
+    ("v", 1, 0),
+    ("x", 3, 0, 0, 0),
+    ("m", 2, 1),
+    ("w", 1, 1, 0, 1),
+    ("g", 1, 0),
+    ("m", 2, 0),
+    ("x", 3, 1, 0, 0),
+    ("g", 1, 1),
+    ("s", 2, 0),
+    ("z", 1),
+    ("y", 1, 0, 0),
+    ("c", 1),
+    ("s", 2, 1),
+    ("y", 1, 1, 0),
+    ("x", 3, 1, 1, 0),
+    ("x", 3, 0, 1, 0),
+    ("x", 3, 2, 1, 0),
+    ("m", 2, 3),
+    ("w", 1, 1, 1, 1),
+    ("m", 2, 2),
+    ("q", 3, 1, 0, 512),
+    ("x", 3, 2, 0, 0),
+    ("q", 3, 0, 0, 512),
+    ("s", 2, 3),
+    ("s", 2, 2),
+    ("q", 3, 2, 0, 512),
+    ("y", 1, 3, 0),
+    ("y", 1, 2, 0),
+    ("v", 1, 1),
+    ("y", 2, 2, 0),
+    ("y", 2, 0, 0),
+    ("m", 3, 1),
+    ("g", 2, 1),
+    ("m", 3, 2),
+    ("w", 1, 2, 1, 1),
+    ("g", 2, 0),
+    ("w", 1, 2, 0, 1),
+    ("m", 3, 0),
+    ("s", 3, 0),
+    ("v", 1, 2),
+    ("s", 3, 1),
+    ("s", 3, 2),
+    ("z", 2),
+    ("y", 2, 3, 0),
+    ("y", 2, 1, 0),
+    ("c", 2),
+    ("m", 3, 3),
+    ("s", 3, 3),
+    ("m", 4, 1),
+    ("g", 3, 0),
+    ("m", 4, 0),
+    ("g", 3, 1),
+    ("m", 4, 2),
+    ("s", 4, 1),
+    ("s", 4, 2),
+    ("s", 4, 0),
+    ("z", 3),
+    ("m", 4, 3),
+    ("y", 3, 1, 0),
+    ("y", 3, 3, 0),
+    ("y", 3, 2, 0),
+    ("c", 3),
+    ("s", 4, 3),
+    ("e", 0, 0, 2048),
+    ("y", 3, 0, 0),
+    ("m", 5, 1),
+    ("g", 4, 0),
+    ("m", 5, 0),
+    ("g", 4, 1),
+    ("m", 5, 2),
+    ("s", 5, 1),
+    ("s", 5, 2),
+    ("s", 5, 0),
+    ("z", 4),
+    ("m", 5, 3),
+    ("y", 4, 1, 0),
+    ("y", 4, 3, 0),
+    ("y", 4, 2, 0),
+    ("c", 4),
+    ("s", 5, 3),
+    ("y", 4, 0, 0),
+    ("m", 6, 1),
+    ("g", 5, 0),
+    ("m", 6, 0),
+    ("g", 5, 1),
+    ("m", 6, 2),
+    ("s", 6, 1),
+    ("s", 6, 2),
+    ("s", 6, 0),
+    ("z", 5),
+    ("m", 6, 3),
+    ("y", 5, 1, 0),
+    ("y", 5, 3, 0),
+    ("y", 5, 2, 0),
+    ("c", 5),
+    ("s", 6, 3),
+    ("y", 5, 0, 0),
+    ("m", 7, 3),
+    ("m", 7, 2),
+    ("m", 7, 1),
+    ("m", 7, 0),
+    ("y", 6, 3, 0),
+    ("s", 7, 3),
+    ("y", 6, 1, 0),
+    ("g", 6, 0),
+    ("s", 7, 0),
+    ("s", 7, 2),
+    ("g", 6, 1),
+    ("y", 6, 0, 0),
+    ("s", 7, 1),
+    ("z", 6),
+    ("c", 6),
+    ("y", 6, 2, 0),
+    ("g", 7, 0),
+    ("g", 7, 1),
+    ("m", 8, 0),
+    ("m", 8, 2),
+    ("s", 8, 0),
+    ("z", 7),
+    ("c", 7),
+    ("y", 7, 1, 0),
+    ("m", 8, 1),
+    ("s", 8, 2),
+    ("e", 1, 0, 1792),
+    ("s", 8, 1),
+    ("m", 8, 3),
+    ("y", 7, 0, 0),
+    ("s", 8, 3),
+    ("y", 8, 1, 0),
+    ("g", 8, 0),
+    ("g", 8, 1),
+    ("y", 8, 0, 0),
+    ("z", 8),
+    ("e", 1, 1792, 256),
+    ("c", 8),
+)
 
 
 def tile_router_hidden_tanh_g1_kernel(tc, x, w_hidden, b_hidden, gain, inv_temp, out_0, out_1, out_2):
@@ -73,18 +275,13 @@ def tile_router_hidden_tanh_g1_kernel(tc, x, w_hidden, b_hidden, gain, inv_temp,
         x_words = {}
         w_raw = {}
 
-        def load_x_pass(b, c):
-            raw = keep.tile([P, BLOCK // P, K_PASS], BF16, name="x_raw%d_%d" % (b, c))
-            rows = x[b * BLOCK : (b + 1) * BLOCK, c * K_PASS : (c + 1) * K_PASS]
+        def load_x(pair, pairs, c0, passes):
+            raw = keep.tile([P, 2 * pairs, passes * K_PASS], BF16, name="x_raw%d_%d" % (pair, c0))
+            rows = x[pair * 2 * P : (pair + pairs) * 2 * P, c0 * K_PASS : (c0 + passes) * K_PASS]
             nc.sync.dma_start(out=raw[:], in_=rows.rearrange("(j p) k -> p j k", p=P))
-            x_words[b, c] = raw[:].bitcast(F32)
-
-        def load_x_block(b):
-            raw = keep.tile([P, BLOCK // P, MODEL], BF16, name="x_raw%d" % b)
-            rows = x[b * BLOCK : (b + 1) * BLOCK, :]
-            nc.sync.dma_start(out=raw[:], in_=rows.rearrange("(j p) k -> p j k", p=P))
-            for c in range(PASSES):
-                x_words[b, c] = raw[:, :, c * K_PASS : (c + 1) * K_PASS].bitcast(F32)
+            for j in range(2 * pairs):
+                for c in range(passes):
+                    x_words[2 * pair + j, c0 + c] = raw[:, j, c * K_PASS : (c + 1) * K_PASS].bitcast(F32)
 
         def load_w(g, c):
             raw = keep.tile([P, PACK, K_PASS], BF16, name="w_raw%d_%d" % (g, c))
@@ -92,16 +289,11 @@ def tile_router_hidden_tanh_g1_kernel(tc, x, w_hidden, b_hidden, gain, inv_temp,
             nc.sync.dma_start(out=raw[:], in_=rows.rearrange("(p j) n -> p j n", j=PACK))
             w_raw[g, c] = raw
 
-        for c in range(PASSES):
-            load_x_pass(0, c)
-            load_w(0, c)
-        for c in range(PASSES):
-            load_x_pass(1, c)
-        load_w(1, 0)
-        load_x_block(2)
-        load_w(1, 1)
-        load_w(1, 2)
-        load_x_block(3)
+        for load in LOADS:
+            if len(load) == 2:
+                load_w(*load)
+            else:
+                load_x(*load)
 
         temp_all = keep.tile([P, TOKENS], BF16)
         temp_pairs = temp_rows[:].bitcast(F32)
@@ -127,26 +319,30 @@ def tile_router_hidden_tanh_g1_kernel(tc, x, w_hidden, b_hidden, gain, inv_temp,
         hidden = {}
         y_turned = {}
         y_grouped = {}
+        y_codes = {}
+        open_banks = {}
 
         def turn_x(b, c, half, engine):
-            if half == 0:
-                x_grouped[b, c] = work.tile([P, BLOCK * PACK], BF16, name="x_grouped", bufs=3, align_bytes=64)
+            if (b, c) not in x_grouped:
+                x_grouped[b, c] = work.tile([P, BLOCK * PACK], BF16, name="x_grouped", bufs=4, align_bytes=64)
             number, bank = take_bank()
             for jj in range(2):
                 for u in range(2):
                     columns = slice(2 * P * u + P * jj, 2 * P * u + P * (jj + 1))
-                    nc.tensor.transpose(bank[:, columns], x_words[b, c][:, 2 * half + jj, u : 2 * P : 2], ident[:])
+                    nc.tensor.transpose(bank[:, columns], x_words[4 * b + 2 * half + jj, c][:, u : 2 * P : 2], ident[:])
             bank_queue.append(number)
             target = x_grouped[b, c][:].bitcast(F32)[:, BLOCK * half : BLOCK * (half + 1)]
             copy_on(engine, target.rearrange("p (n u) -> p n u", u=2), bank[:].rearrange("p (u n) -> p n u", u=2))
 
-        def quantize_x(b, c):
+        def quantize_x(b, c, start, count):
             nc.vector.quantize_mx(
-                out=x_codes[b][:, c, :].bitcast(FP8X4), scales=x_scales[b][:, c, :], in_=x_grouped[b, c][:]
+                out=x_codes[b][:, c, start : start + count].bitcast(FP8X4),
+                scales=x_scales[b][:, c, start : start + count],
+                in_=x_grouped[b, c][:, start * PACK : (start + count) * PACK],
             )
 
         def group_w(g, c, half, engine):
-            if half == 0:
+            if (g, c) not in w_grouped:
                 w_grouped[g, c] = work.tile([P, K_PASS * PACK], BF16, name="w_grouped", bufs=3, align_bytes=64)
             target = w_grouped[g, c][:].rearrange("p (t m j) -> p t m j", t=PACK, j=PACK)
             source = w_raw[g, c][:].rearrange("p j (m t) -> p t m j", t=PACK)
@@ -188,7 +384,7 @@ def tile_router_hidden_tanh_g1_kernel(tc, x, w_hidden, b_hidden, gain, inv_temp,
 
         def scale_y(unit, t):
             g, first, count = unit
-            if t == 0:
+            if unit not in y_turned:
                 y_turned[unit] = work.tile([P, PACK, BLOCK], F32, name="y_turned", bufs=3)
             nc.vector.scalar_tensor_tensor(
                 out=y_turned[unit][:, t, 0:count],
@@ -199,23 +395,29 @@ def tile_router_hidden_tanh_g1_kernel(tc, x, w_hidden, b_hidden, gain, inv_temp,
                 op1=MULT,
             )
 
-        def group_y(unit):
+        def group_y(unit, half):
             g, first, count = unit
-            y_grouped[unit] = work.tile([P, BLOCK * PACK], BF16, name="y_grouped", bufs=2, align_bytes=64)
+            if unit not in y_grouped:
+                y_grouped[unit] = work.tile([P, BLOCK * PACK], BF16, name="y_grouped", bufs=2, align_bytes=64)
+            tokens = slice(half * count // 2, (half + 1) * count // 2)
+            target = y_grouped[unit][:].rearrange("p (n t) -> p n t", t=PACK)[:, tokens, :]
             nc.vector.tensor_copy(
-                out=y_grouped[unit][:, 0 : count * PACK].rearrange("p (n t) -> p n t", t=PACK),
-                in_=y_turned[unit][:, :, 0:count].rearrange("p t n -> p n t"),
+                out=target.rearrange("p (c i) t -> p c t i", i=2),
+                in_=y_turned[unit][:, :, tokens].rearrange("p t (c i) -> p c t i", i=2),
             )
 
         def quantize_y(unit):
             g, first, count = unit
-            y_codes = work.tile([P, BLOCK], U32, name="y_codes", bufs=3, align_bytes=64)
+            y_codes[unit] = work.tile([P, BLOCK], U32, name="y_codes", bufs=3, align_bytes=64)
             nc.vector.quantize_mx(
-                out=y_codes[:, 0:count].bitcast(FP8X4),
+                out=y_codes[unit][:, 0:count].bitcast(FP8X4),
                 scales=y_scales[g][:, first : first + count],
                 in_=y_grouped[unit][:, 0 : count * PACK],
             )
-            nc.sync.dma_start(out=words_out[g, :, first : first + count], in_=y_codes[:, 0:count].bitcast(I32))
+
+        def store_codes(unit):
+            g, first, count = unit
+            nc.sync.dma_start(out=words_out[g, :, first : first + count], in_=y_codes[unit][:, 0:count].bitcast(I32))
 
         def store_scales(g, first, count):
             columns = slice(first // 4, (first + count) // 4)
@@ -240,85 +442,39 @@ def tile_router_hidden_tanh_g1_kernel(tc, x, w_hidden, b_hidden, gain, inv_temp,
             row = first + j * P
             nc.sync.dma_start(out=out_0[row : row + P, g * K_PASS : (g + 1) * K_PASS], in_=y_rows[:])
 
-        units = [(g, b * BLOCK, BLOCK) for g in range(GROUPS) for b in range(BLOCKS)][:-1]
-        first = TOKENS - BLOCK
-        for count in LAST_PIECES:
-            units.append((GROUPS - 1, first, count))
-            first += count
+        def open_pass(unit, t, c):
+            if c == 0:
+                open_banks[unit, t] = take_bank()
+            number, bank = open_banks[unit, t]
+            mx_pass(unit, t, c, bank)
+            if c == PASSES - 1:
+                bank_queue.append(number)
+                activate(unit, t, bank)
 
-        head = units[0]
-        open_banks = []
-        for c in range(PASSES):
-            turn_x(0, c, 0, "scalar")
-            turn_x(0, c, 1, "scalar")
-            if c > 0:
-                for t in range(PACK):
-                    if c == 1:
-                        open_banks.append(take_bank())
-                    mx_pass(head, t, c - 1, open_banks[t][1])
-            group_w(0, c, 0, "vector")
-            group_w(0, c, 1, "scalar")
-            quantize_x(0, c)
-            quantize_w(0, c)
-        turn_x(1, 0, 0, HEAD_X[0])
-        turn_x(1, 0, 1, HEAD_X[1])
-        for t in range(PACK):
-            mx_pass(head, t, PASSES - 1, open_banks[t][1])
-            bank_queue.append(open_banks[t][0])
-            activate(head, t, open_banks[t][1])
-        quantize_x(1, 0)
-        turn_x(1, 1, 0, HEAD_X[2])
-        turn_x(1, 1, 1, HEAD_X[3])
-        scale_y(head, 0)
-        quantize_x(1, 1)
-        turn_x(1, 2, 0, HEAD_X[4])
-        turn_x(1, 2, 1, HEAD_X[5])
-        scale_y(head, 1)
-        quantize_x(1, 2)
-        scale_y(head, 2)
-        scale_y(head, 3)
-
-        for i in range(1, len(units)):
-            unit, before = units[i], units[i - 1]
-            tiles = before[2] // P
-            if i < BLOCKS - 1:
-                steps = PLAN_X
-            elif i == BLOCKS - 1:
-                steps = PLAN_W
-            elif unit[2] == BLOCK:
-                steps = PLAN_Y
-            else:
-                steps = PLAN_T
-            for step in steps.split():
-                kind, n = step[0], int(step[1])
-                engine = "vector" if len(step) > 2 else "scalar"
-                if kind == "m":
-                    multiply(unit, n)
-                elif kind == "s":
-                    scale_y(unit, n)
-                elif kind == "x":
-                    turn_x(i + 1, n // 2, n % 2, engine)
-                elif kind == "q":
-                    quantize_x(i + 1, n)
-                elif kind == "y":
-                    if n < tiles:
-                        turn_y(before, n, engine)
-                elif kind == "g":
-                    group_y(before)
-                elif kind == "z":
-                    quantize_y(before)
-                    if before[1] + before[2] == TOKENS:
-                        store_scales(before[0], 0, TOKENS)
-                    if i == len(units) - 1:
-                        store_scales(unit[0], 0, unit[1])
-                elif kind == "w":
-                    group_w(1, i - 1, n, "vector")
-                elif kind == "v":
-                    quantize_w(1, i - 1)
-
-        last = units[-1]
-        group_y(last)
-        for j in range(last[2] // P):
-            turn_y(last, j, "scalar")
-        quantize_y(last)
-        store_scales(last[0], last[1], last[2])
+        engines = ("scalar", "vector")
+        for step in PLAN:
+            kind = step[0]
+            if kind == "p":
+                open_pass(UNITS[step[1]], step[2], step[3])
+            elif kind == "m":
+                multiply(UNITS[step[1]], step[2])
+            elif kind == "s":
+                scale_y(UNITS[step[1]], step[2])
+            elif kind == "x":
+                turn_x(step[1], step[2], step[3], engines[step[4]])
+            elif kind == "q":
+                quantize_x(*step[1:])
+            elif kind == "y":
+                turn_y(UNITS[step[1]], step[2], engines[step[3]])
+            elif kind == "g":
+                group_y(UNITS[step[1]], step[2])
+            elif kind == "z":
+                quantize_y(UNITS[step[1]])
+            elif kind == "c":
+                store_codes(UNITS[step[1]])
+            elif kind == "e":
+                store_scales(*step[1:])
+            elif kind == "w":
+                group_w(step[1], step[2], step[3], engines[step[4]])
+            elif kind == "v":
+                quantize_w(step[1], step[2])

@@ -23,214 +23,230 @@ GROUPS = HIDDEN // K_PASS
 BLOCK = 512
 BLOCKS = TOKENS // BLOCK
 BANKS = 8
-LOADS = ((0, 2, 0, 1), (0, 0), (0, 2, 1, 1), (0, 1), (0, 2, 2, 1), (0, 2), (2, 2, 0, 1), (2, 2, 1, 1), (2, 2, 2, 1), (4, 2, 0, 3), (1, 0), (6, 2, 0, 3), (1, 1), (1, 2))
-UNITS = ((0, 0, 512), (0, 512, 512), (0, 1024, 512), (0, 1536, 512), (1, 0, 512), (1, 512, 512), (1, 1024, 512), (1, 1536, 256), (1, 1792, 256))
+SPLIT = ()
+LOADS = ((0, 1, 0, 3), (0, 0), (0, 1), (1, 1, 0, 3), (0, 2), (2, 1, 0, 3), (3, 1, 0, 3), (4, 2, 0, 3), (1, 0), (6, 2, 0, 3), (1, 1), (1, 2))
+UNITS = ((0, 0, 256), (0, 256, 256), (0, 512, 512), (0, 1024, 512), (0, 1536, 512), (1, 0, 512), (1, 512, 512), (1, 1024, 512), (1, 1536, 256), (1, 1792, 256))
 PLAN = (
-    ("x", 0, 0, 1, 0),
-    ("w", 0, 0, 1, 0),
-    ("w", 0, 0, 0, 1),
     ("x", 0, 0, 0, 0),
-    ("w", 0, 1, 1, 0),
+    ("w", 0, 0, 0, 0),
+    ("q", 0, 0, 0, 256),
+    ("w", 0, 0, 1, 1),
     ("v", 0, 0),
-    ("w", 0, 1, 0, 0),
-    ("q", 0, 0, 0, 512),
-    ("x", 0, 1, 0, 1),
-    ("x", 0, 1, 1, 1),
-    ("q", 0, 1, 0, 512),
-    ("v", 0, 1),
-    ("w", 0, 2, 0, 1),
+    ("x", 0, 1, 0, 0),
+    ("q", 0, 1, 0, 256),
+    ("x", 0, 2, 0, 0),
+    ("w", 0, 1, 0, 1),
     ("p", 0, 0, 0),
     ("p", 0, 1, 0),
     ("p", 0, 2, 0),
     ("p", 0, 3, 0),
+    ("w", 0, 1, 1, 0),
+    ("v", 0, 1),
+    ("w", 0, 2, 0, 1),
     ("w", 0, 2, 1, 0),
-    ("x", 0, 2, 1, 0),
-    ("x", 0, 2, 0, 1),
+    ("q", 0, 2, 0, 256),
+    ("v", 0, 2),
+    ("x", 0, 0, 1, 0),
+    ("x", 0, 1, 1, 0),
+    ("x", 0, 2, 1, 1),
+    ("q", 0, 0, 256, 256),
     ("p", 0, 0, 1),
     ("p", 0, 1, 1),
     ("p", 0, 2, 1),
     ("p", 0, 3, 1),
-    ("q", 0, 2, 0, 512),
-    ("x", 1, 0, 0, 0),
-    ("v", 0, 2),
-    ("x", 1, 0, 1, 1),
-    ("p", 0, 1, 2),
     ("p", 0, 0, 2),
-    ("q", 1, 0, 0, 512),
+    ("q", 0, 1, 256, 256),
+    ("q", 0, 2, 256, 256),
     ("s", 0, 0),
-    ("x", 1, 2, 1, 0),
-    ("p", 0, 3, 2),
-    ("s", 0, 1),
-    ("x", 1, 1, 0, 0),
-    ("x", 1, 1, 1, 1),
+    ("p", 0, 1, 2),
     ("p", 0, 2, 2),
-    ("s", 0, 3),
-    ("x", 1, 2, 0, 0),
-    ("q", 1, 1, 0, 512),
-    ("q", 1, 2, 0, 512),
+    ("s", 0, 1),
+    ("p", 0, 3, 2),
     ("s", 0, 2),
-    ("x", 2, 0, 0, 0),
-    ("m", 1, 1),
-    ("w", 1, 0, 0, 1),
+    ("s", 0, 3),
+    ("x", 1, 0, 0, 0),
     ("g", 0, 0),
+    ("x", 1, 0, 1, 0),
     ("m", 1, 0),
-    ("x", 2, 1, 0, 0),
     ("g", 0, 1),
-    ("s", 1, 0),
+    ("x", 1, 1, 0, 1),
+    ("x", 1, 1, 1, 0),
     ("z", 0),
+    ("q", 1, 0, 0, 512),
     ("y", 0, 0, 0),
+    ("s", 1, 0),
+    ("m", 1, 1),
+    ("x", 1, 2, 0, 0),
     ("c", 0),
-    ("s", 1, 1),
+    ("q", 1, 1, 0, 512),
+    ("x", 1, 2, 1, 0),
+    ("q", 1, 2, 0, 512),
     ("y", 0, 1, 0),
-    ("x", 2, 1, 1, 0),
-    ("x", 2, 0, 1, 0),
-    ("x", 2, 2, 1, 0),
-    ("m", 1, 3),
-    ("w", 1, 0, 1, 1),
     ("m", 1, 2),
-    ("q", 2, 1, 0, 512),
-    ("x", 2, 2, 0, 0),
-    ("q", 2, 0, 0, 512),
-    ("s", 1, 3),
+    ("s", 1, 1),
+    ("m", 1, 3),
     ("s", 1, 2),
-    ("q", 2, 2, 0, 512),
-    ("y", 0, 3, 0),
-    ("y", 0, 2, 0),
-    ("v", 1, 0),
-    ("x", 3, 0, 0, 0),
-    ("m", 2, 1),
-    ("w", 1, 1, 0, 1),
-    ("g", 1, 0),
+    ("s", 1, 3),
+    ("x", 2, 0, 0, 1),
+    ("x", 2, 0, 1, 1),
+    ("w", 1, 0, 0, 0),
+    ("w", 1, 0, 1, 0),
     ("m", 2, 0),
-    ("x", 3, 1, 0, 0),
-    ("g", 1, 1),
-    ("s", 2, 0),
-    ("z", 1),
+    ("q", 2, 0, 0, 512),
+    ("x", 2, 1, 0, 0),
+    ("v", 1, 0),
+    ("g", 1, 0),
+    ("x", 2, 1, 1, 1),
     ("y", 1, 0, 0),
-    ("c", 1),
-    ("s", 2, 1),
+    ("m", 2, 1),
+    ("s", 2, 0),
+    ("x", 2, 2, 0, 0),
+    ("x", 2, 2, 1, 0),
+    ("g", 1, 1),
+    ("q", 2, 1, 0, 512),
     ("y", 1, 1, 0),
-    ("x", 3, 1, 1, 0),
-    ("x", 3, 0, 1, 0),
-    ("x", 3, 2, 1, 0),
-    ("m", 2, 3),
-    ("w", 1, 1, 1, 1),
+    ("z", 1),
+    ("c", 1),
     ("m", 2, 2),
-    ("q", 3, 1, 0, 512),
-    ("x", 3, 2, 0, 0),
-    ("q", 3, 0, 0, 512),
-    ("s", 2, 3),
+    ("q", 2, 2, 0, 512),
+    ("m", 2, 3),
+    ("s", 2, 1),
     ("s", 2, 2),
-    ("q", 3, 2, 0, 512),
-    ("y", 1, 3, 0),
-    ("y", 1, 2, 0),
-    ("v", 1, 1),
-    ("y", 2, 2, 0),
-    ("y", 2, 0, 0),
-    ("m", 3, 1),
-    ("g", 2, 1),
-    ("m", 3, 2),
-    ("w", 1, 2, 1, 1),
+    ("s", 2, 3),
+    ("w", 1, 1, 0, 1),
     ("g", 2, 0),
-    ("w", 1, 2, 0, 1),
+    ("x", 3, 0, 0, 0),
+    ("w", 1, 1, 1, 1),
+    ("x", 3, 0, 1, 0),
     ("m", 3, 0),
     ("s", 3, 0),
-    ("v", 1, 2),
+    ("q", 3, 0, 0, 512),
+    ("x", 3, 1, 0, 0),
+    ("v", 1, 1),
+    ("x", 3, 1, 1, 0),
+    ("y", 2, 0, 0),
+    ("m", 3, 1),
+    ("x", 3, 2, 0, 0),
     ("s", 3, 1),
-    ("s", 3, 2),
-    ("z", 2),
-    ("y", 2, 3, 0),
+    ("x", 3, 2, 1, 0),
+    ("q", 3, 1, 0, 512),
     ("y", 2, 1, 0),
+    ("m", 3, 2),
+    ("g", 2, 1),
+    ("y", 2, 2, 0),
+    ("q", 3, 2, 0, 512),
+    ("z", 2),
     ("c", 2),
+    ("y", 2, 3, 0),
+    ("s", 3, 2),
     ("m", 3, 3),
     ("s", 3, 3),
-    ("m", 4, 1),
-    ("g", 3, 0),
+    ("w", 1, 2, 0, 0),
     ("m", 4, 0),
+    ("w", 1, 2, 1, 1),
+    ("g", 3, 0),
+    ("m", 4, 1),
     ("g", 3, 1),
     ("m", 4, 2),
+    ("m", 4, 3),
+    ("s", 4, 0),
+    ("v", 1, 2),
+    ("y", 3, 0, 1),
     ("s", 4, 1),
     ("s", 4, 2),
-    ("s", 4, 0),
-    ("z", 3),
-    ("m", 4, 3),
     ("y", 3, 1, 0),
-    ("y", 3, 3, 0),
     ("y", 3, 2, 0),
-    ("c", 3),
     ("s", 4, 3),
-    ("e", 0, 0, 2048),
-    ("y", 3, 0, 0),
-    ("m", 5, 1),
+    ("y", 3, 3, 0),
+    ("z", 3),
+    ("c", 3),
     ("g", 4, 0),
     ("m", 5, 0),
-    ("g", 4, 1),
-    ("m", 5, 2),
-    ("s", 5, 1),
-    ("s", 5, 2),
+    ("m", 5, 1),
     ("s", 5, 0),
-    ("z", 4),
+    ("m", 5, 2),
+    ("g", 4, 1),
+    ("s", 5, 1),
     ("m", 5, 3),
-    ("y", 4, 1, 0),
-    ("y", 4, 3, 0),
-    ("y", 4, 2, 0),
-    ("c", 4),
-    ("s", 5, 3),
+    ("s", 5, 2),
     ("y", 4, 0, 0),
-    ("m", 6, 1),
+    ("y", 4, 1, 0),
+    ("y", 4, 2, 0),
+    ("s", 5, 3),
+    ("z", 4),
+    ("y", 4, 3, 0),
+    ("c", 4),
+    ("e", 0, 0, 2048),
     ("g", 5, 0),
     ("m", 6, 0),
-    ("g", 5, 1),
-    ("m", 6, 2),
-    ("s", 6, 1),
-    ("s", 6, 2),
+    ("m", 6, 1),
     ("s", 6, 0),
-    ("z", 5),
+    ("m", 6, 2),
+    ("g", 5, 1),
+    ("s", 6, 1),
     ("m", 6, 3),
-    ("y", 5, 1, 0),
-    ("y", 5, 3, 0),
-    ("y", 5, 2, 0),
-    ("c", 5),
-    ("s", 6, 3),
+    ("s", 6, 2),
     ("y", 5, 0, 0),
-    ("m", 7, 3),
-    ("m", 7, 2),
-    ("m", 7, 1),
-    ("m", 7, 0),
-    ("y", 6, 3, 0),
-    ("s", 7, 3),
-    ("y", 6, 1, 0),
+    ("y", 5, 1, 0),
+    ("y", 5, 2, 0),
+    ("s", 6, 3),
+    ("z", 5),
+    ("y", 5, 3, 0),
+    ("c", 5),
     ("g", 6, 0),
+    ("m", 7, 0),
+    ("m", 7, 1),
     ("s", 7, 0),
-    ("s", 7, 2),
+    ("m", 7, 2),
     ("g", 6, 1),
-    ("y", 6, 0, 0),
     ("s", 7, 1),
-    ("z", 6),
-    ("c", 6),
+    ("m", 7, 3),
+    ("s", 7, 2),
+    ("y", 6, 0, 0),
+    ("y", 6, 1, 0),
     ("y", 6, 2, 0),
+    ("s", 7, 3),
+    ("z", 6),
+    ("y", 6, 3, 0),
+    ("c", 6),
     ("g", 7, 0),
-    ("g", 7, 1),
     ("m", 8, 0),
-    ("m", 8, 2),
-    ("s", 8, 0),
-    ("z", 7),
-    ("c", 7),
-    ("y", 7, 1, 0),
     ("m", 8, 1),
-    ("s", 8, 2),
-    ("e", 1, 0, 1792),
+    ("s", 8, 0),
     ("s", 8, 1),
+    ("m", 8, 2),
+    ("g", 7, 1),
+    ("s", 8, 2),
     ("m", 8, 3),
-    ("y", 7, 0, 0),
     ("s", 8, 3),
-    ("y", 8, 1, 0),
+    ("z", 7),
+    ("y", 7, 0, 0),
+    ("y", 7, 1, 0),
+    ("y", 7, 2, 0),
+    ("c", 7),
+    ("y", 7, 3, 0),
+    ("m", 9, 0),
     ("g", 8, 0),
+    ("m", 9, 1),
     ("g", 8, 1),
-    ("y", 8, 0, 0),
+    ("s", 9, 0),
+    ("m", 9, 2),
     ("z", 8),
-    ("e", 1, 1792, 256),
+    ("s", 9, 1),
+    ("s", 9, 2),
     ("c", 8),
+    ("m", 9, 3),
+    ("y", 8, 0, 0),
+    ("y", 8, 1, 0),
+    ("s", 9, 3),
+    ("e", 1, 0, 1792),
+    ("g", 9, 0),
+    ("y", 9, 0, 0),
+    ("g", 9, 1),
+    ("z", 9),
+    ("c", 9),
+    ("y", 9, 1, 0),
+    ("e", 1, 1792, 256),
 )
 
 
@@ -346,7 +362,8 @@ def tile_router_hidden_tanh_g1_kernel(tc, x, w_hidden, b_hidden, gain, inv_temp,
                 w_grouped[g, c] = work.tile([P, K_PASS * PACK], BF16, name="w_grouped", bufs=3, align_bytes=64)
             target = w_grouped[g, c][:].rearrange("p (t m j) -> p t m j", t=PACK, j=PACK)
             source = w_raw[g, c][:].rearrange("p j (m t) -> p t m j", t=PACK)
-            copy_on(engine, target[:, 2 * half : 2 * half + 2], source[:, 2 * half : 2 * half + 2])
+            part = slice(2 * half, 2 * half + 2) if half < 2 else slice(0, PACK)
+            copy_on(engine, target[:, part], source[:, part])
 
         def quantize_w(g, c):
             nc.vector.quantize_mx(
@@ -399,7 +416,7 @@ def tile_router_hidden_tanh_g1_kernel(tc, x, w_hidden, b_hidden, gain, inv_temp,
             g, first, count = unit
             if unit not in y_grouped:
                 y_grouped[unit] = work.tile([P, BLOCK * PACK], BF16, name="y_grouped", bufs=2, align_bytes=64)
-            tokens = slice(half * count // 2, (half + 1) * count // 2)
+            tokens = slice(half * count // 2, (half + 1) * count // 2) if half < 2 else slice(0, count)
             target = y_grouped[unit][:].rearrange("p (n t) -> p n t", t=PACK)[:, tokens, :]
             nc.vector.tensor_copy(
                 out=target.rearrange("p (c i) t -> p c t i", i=2),
@@ -451,6 +468,20 @@ def tile_router_hidden_tanh_g1_kernel(tc, x, w_hidden, b_hidden, gain, inv_temp,
                 bank_queue.append(number)
                 activate(unit, t, bank)
 
+        def warm_up(count):
+            number, bank = take_bank()
+            for n in range(count):
+                nc.tensor.matmul_mx(
+                    out=bank[:],
+                    lhsT=w_codes[0][:, 0, 0:P].bitcast(FP8X4),
+                    lhsT_scale=w_scales[0][:, 0, 0:P],
+                    rhs=w_codes[0][:, 0, :].bitcast(FP8X4),
+                    rhs_scale=w_scales[0][:, 0, :],
+                    start=True,
+                    stop=True,
+                )
+            bank_queue.append(number)
+
         engines = ("scalar", "vector")
         for step in PLAN:
             kind = step[0]
@@ -476,5 +507,7 @@ def tile_router_hidden_tanh_g1_kernel(tc, x, w_hidden, b_hidden, gain, inv_temp,
                 store_scales(*step[1:])
             elif kind == "w":
                 group_w(step[1], step[2], step[3], engines[step[4]])
+            elif kind == "d":
+                warm_up(step[1])
             elif kind == "v":
                 quantize_w(step[1], step[2])

@@ -21,232 +21,16 @@ K_PASS = P * PACK
 PASSES = MODEL // K_PASS
 GROUPS = HIDDEN // K_PASS
 BLOCK = 512
+HALF = BLOCK // 2
 BLOCKS = TOKENS // BLOCK
 BANKS = 8
-SPLIT = ()
-LOADS = ((0, 1, 0, 3), (0, 0), (0, 1), (1, 1, 0, 3), (0, 2), (2, 1, 0, 3), (3, 1, 0, 3), (4, 2, 0, 3), (1, 0), (6, 2, 0, 3), (1, 1), (1, 2))
-UNITS = ((0, 0, 256), (0, 256, 256), (0, 512, 512), (0, 1024, 512), (0, 1536, 512), (1, 0, 512), (1, 512, 512), (1, 1024, 512), (1, 1536, 256), (1, 1792, 256))
-PLAN = (
-    ("x", 0, 0, 0, 0),
-    ("w", 0, 0, 0, 0),
-    ("q", 0, 0, 0, 256),
-    ("w", 0, 0, 1, 1),
-    ("v", 0, 0),
-    ("x", 0, 1, 0, 0),
-    ("q", 0, 1, 0, 256),
-    ("x", 0, 2, 0, 0),
-    ("w", 0, 1, 0, 1),
-    ("p", 0, 0, 0),
-    ("p", 0, 1, 0),
-    ("p", 0, 2, 0),
-    ("p", 0, 3, 0),
-    ("w", 0, 1, 1, 0),
-    ("v", 0, 1),
-    ("w", 0, 2, 0, 1),
-    ("w", 0, 2, 1, 0),
-    ("q", 0, 2, 0, 256),
-    ("v", 0, 2),
-    ("x", 0, 0, 1, 0),
-    ("x", 0, 1, 1, 0),
-    ("x", 0, 2, 1, 1),
-    ("q", 0, 0, 256, 256),
-    ("p", 0, 0, 1),
-    ("p", 0, 1, 1),
-    ("p", 0, 2, 1),
-    ("p", 0, 3, 1),
-    ("p", 0, 0, 2),
-    ("q", 0, 1, 256, 256),
-    ("q", 0, 2, 256, 256),
-    ("s", 0, 0),
-    ("p", 0, 1, 2),
-    ("p", 0, 2, 2),
-    ("s", 0, 1),
-    ("p", 0, 3, 2),
-    ("s", 0, 2),
-    ("s", 0, 3),
-    ("x", 1, 0, 0, 0),
-    ("g", 0, 0),
-    ("x", 1, 0, 1, 0),
-    ("m", 1, 0),
-    ("g", 0, 1),
-    ("x", 1, 1, 0, 1),
-    ("x", 1, 1, 1, 0),
-    ("z", 0),
-    ("q", 1, 0, 0, 512),
-    ("y", 0, 0, 0),
-    ("s", 1, 0),
-    ("m", 1, 1),
-    ("x", 1, 2, 0, 0),
-    ("c", 0),
-    ("q", 1, 1, 0, 512),
-    ("x", 1, 2, 1, 0),
-    ("q", 1, 2, 0, 512),
-    ("y", 0, 1, 0),
-    ("m", 1, 2),
-    ("s", 1, 1),
-    ("m", 1, 3),
-    ("s", 1, 2),
-    ("s", 1, 3),
-    ("x", 2, 0, 0, 1),
-    ("x", 2, 0, 1, 1),
-    ("w", 1, 0, 0, 0),
-    ("w", 1, 0, 1, 0),
-    ("m", 2, 0),
-    ("q", 2, 0, 0, 512),
-    ("x", 2, 1, 0, 0),
-    ("v", 1, 0),
-    ("g", 1, 0),
-    ("x", 2, 1, 1, 1),
-    ("y", 1, 0, 0),
-    ("m", 2, 1),
-    ("s", 2, 0),
-    ("x", 2, 2, 0, 0),
-    ("x", 2, 2, 1, 0),
-    ("g", 1, 1),
-    ("q", 2, 1, 0, 512),
-    ("y", 1, 1, 0),
-    ("z", 1),
-    ("c", 1),
-    ("m", 2, 2),
-    ("q", 2, 2, 0, 512),
-    ("m", 2, 3),
-    ("s", 2, 1),
-    ("s", 2, 2),
-    ("s", 2, 3),
-    ("w", 1, 1, 0, 1),
-    ("g", 2, 0),
-    ("x", 3, 0, 0, 0),
-    ("w", 1, 1, 1, 1),
-    ("x", 3, 0, 1, 0),
-    ("m", 3, 0),
-    ("s", 3, 0),
-    ("q", 3, 0, 0, 512),
-    ("x", 3, 1, 0, 0),
-    ("v", 1, 1),
-    ("x", 3, 1, 1, 0),
-    ("y", 2, 0, 0),
-    ("m", 3, 1),
-    ("x", 3, 2, 0, 0),
-    ("s", 3, 1),
-    ("x", 3, 2, 1, 0),
-    ("q", 3, 1, 0, 512),
-    ("y", 2, 1, 0),
-    ("m", 3, 2),
-    ("g", 2, 1),
-    ("y", 2, 2, 0),
-    ("q", 3, 2, 0, 512),
-    ("z", 2),
-    ("c", 2),
-    ("y", 2, 3, 0),
-    ("s", 3, 2),
-    ("m", 3, 3),
-    ("s", 3, 3),
-    ("w", 1, 2, 0, 0),
-    ("m", 4, 0),
-    ("w", 1, 2, 1, 1),
-    ("g", 3, 0),
-    ("m", 4, 1),
-    ("g", 3, 1),
-    ("m", 4, 2),
-    ("m", 4, 3),
-    ("s", 4, 0),
-    ("v", 1, 2),
-    ("y", 3, 0, 1),
-    ("s", 4, 1),
-    ("s", 4, 2),
-    ("y", 3, 1, 0),
-    ("y", 3, 2, 0),
-    ("s", 4, 3),
-    ("y", 3, 3, 0),
-    ("z", 3),
-    ("c", 3),
-    ("g", 4, 0),
-    ("m", 5, 0),
-    ("m", 5, 1),
-    ("s", 5, 0),
-    ("m", 5, 2),
-    ("g", 4, 1),
-    ("s", 5, 1),
-    ("m", 5, 3),
-    ("s", 5, 2),
-    ("y", 4, 0, 0),
-    ("y", 4, 1, 0),
-    ("y", 4, 2, 0),
-    ("s", 5, 3),
-    ("z", 4),
-    ("y", 4, 3, 0),
-    ("c", 4),
-    ("e", 0, 0, 2048),
-    ("g", 5, 0),
-    ("m", 6, 0),
-    ("m", 6, 1),
-    ("s", 6, 0),
-    ("m", 6, 2),
-    ("g", 5, 1),
-    ("s", 6, 1),
-    ("m", 6, 3),
-    ("s", 6, 2),
-    ("y", 5, 0, 0),
-    ("y", 5, 1, 0),
-    ("y", 5, 2, 0),
-    ("s", 6, 3),
-    ("z", 5),
-    ("y", 5, 3, 0),
-    ("c", 5),
-    ("g", 6, 0),
-    ("m", 7, 0),
-    ("m", 7, 1),
-    ("s", 7, 0),
-    ("m", 7, 2),
-    ("g", 6, 1),
-    ("s", 7, 1),
-    ("m", 7, 3),
-    ("s", 7, 2),
-    ("y", 6, 0, 0),
-    ("y", 6, 1, 0),
-    ("y", 6, 2, 0),
-    ("s", 7, 3),
-    ("z", 6),
-    ("y", 6, 3, 0),
-    ("c", 6),
-    ("g", 7, 0),
-    ("m", 8, 0),
-    ("m", 8, 1),
-    ("s", 8, 0),
-    ("s", 8, 1),
-    ("m", 8, 2),
-    ("g", 7, 1),
-    ("s", 8, 2),
-    ("m", 8, 3),
-    ("s", 8, 3),
-    ("z", 7),
-    ("y", 7, 0, 0),
-    ("y", 7, 1, 0),
-    ("y", 7, 2, 0),
-    ("c", 7),
-    ("y", 7, 3, 0),
-    ("m", 9, 0),
-    ("g", 8, 0),
-    ("m", 9, 1),
-    ("g", 8, 1),
-    ("s", 9, 0),
-    ("m", 9, 2),
-    ("z", 8),
-    ("s", 9, 1),
-    ("s", 9, 2),
-    ("c", 8),
-    ("m", 9, 3),
-    ("y", 8, 0, 0),
-    ("y", 8, 1, 0),
-    ("s", 9, 3),
-    ("e", 1, 0, 1792),
-    ("g", 9, 0),
-    ("y", 9, 0, 0),
-    ("g", 9, 1),
-    ("z", 9),
-    ("c", 9),
-    ("y", 9, 1, 0),
-    ("e", 1, 1792, 256),
+QUADRANT = 32
+
+UNITS = (
+    [(0, 0, HALF), (0, HALF, HALF)]
+    + [(0, b * BLOCK, BLOCK) for b in range(1, BLOCKS)]
+    + [(1, b * BLOCK, BLOCK) for b in range(BLOCKS - 1)]
+    + [(1, TOKENS - BLOCK, HALF), (1, TOKENS - HALF, HALF)]
 )
 
 
@@ -275,7 +59,8 @@ def tile_router_hidden_tanh_g1_kernel(tc, x, w_hidden, b_hidden, gain, inv_temp,
             else:
                 nc.vector.tensor_copy(out=out, in_=in_)
 
-        temp_rows = keep.tile([P, TOKENS // P], BF16)
+        temps_a_row = TOKENS // P
+        temp_rows = keep.tile([P, temps_a_row], BF16)
         bias = keep.tile([P, GROUPS, PACK], BF16)
         gains = keep.tile([P, GROUPS, PACK], BF16)
         nc.scalar.dma_start(out=temp_rows[:], in_=inv_temp.rearrange("(n j) -> n j", n=P))
@@ -288,16 +73,15 @@ def tile_router_hidden_tanh_g1_kernel(tc, x, w_hidden, b_hidden, gain, inv_temp,
         nc.vector.memset(warm[:, 0:1], 0.0)
         nc.scalar.activation(out=warm[:, 1:2], in_=warm[:, 0:1], func=TANH)
 
-        x_words = {}
+        x_pairs = {}
         w_raw = {}
 
-        def load_x(pair, pairs, c0, passes):
-            raw = keep.tile([P, 2 * pairs, passes * K_PASS], BF16, name="x_raw%d_%d" % (pair, c0))
-            rows = x[pair * 2 * P : (pair + pairs) * 2 * P, c0 * K_PASS : (c0 + passes) * K_PASS]
-            nc.sync.dma_start(out=raw[:], in_=rows.rearrange("(j p) k -> p j k", p=P))
-            for j in range(2 * pairs):
-                for c in range(passes):
-                    x_words[2 * pair + j, c0 + c] = raw[:, j, c * K_PASS : (c + 1) * K_PASS].bitcast(F32)
+        def load_x(first, count):
+            raw = keep.tile([P, count // P, MODEL], BF16, name="x_raw%d" % first)
+            nc.sync.dma_start(out=raw[:], in_=x[first : first + count, :].rearrange("(j p) k -> p j k", p=P))
+            for j in range(count // P):
+                for c in range(PASSES):
+                    x_pairs[first // P + j, c] = raw[:, j, c * K_PASS : (c + 1) * K_PASS].bitcast(F32)
 
         def load_w(g, c):
             raw = keep.tile([P, PACK, K_PASS], BF16, name="w_raw%d_%d" % (g, c))
@@ -305,25 +89,29 @@ def tile_router_hidden_tanh_g1_kernel(tc, x, w_hidden, b_hidden, gain, inv_temp,
             nc.sync.dma_start(out=raw[:], in_=rows.rearrange("(p j) n -> p j n", j=PACK))
             w_raw[g, c] = raw
 
-        for load in LOADS:
-            if len(load) == 2:
-                load_w(*load)
-            else:
-                load_x(*load)
+        load_x(0, HALF)
+        load_w(0, 0)
+        load_w(0, 1)
+        load_x(HALF, HALF)
+        load_w(0, 2)
+        load_x(BLOCK, HALF)
+        load_x(BLOCK + HALF, HALF)
+        load_x(2 * BLOCK, BLOCK)
+        load_w(1, 0)
+        load_x(3 * BLOCK, BLOCK)
+        load_w(1, 1)
+        load_w(1, 2)
 
         temp_all = keep.tile([P, TOKENS], BF16)
         temp_pairs = temp_rows[:].bitcast(F32)
         temp_all_pairs = temp_all[:].bitcast(F32).rearrange("p (n w) -> p n w", n=P)
-        for half in range(2):
+        for w0 in range(0, temps_a_row // 2, PACK):
             number, bank = take_bank()
             for w in range(PACK):
-                column = temp_pairs[:, PACK * half + w : PACK * half + w + 1]
+                column = temp_pairs[:, w0 + w : w0 + w + 1]
                 nc.tensor.transpose(bank[:, w * P : (w + 1) * P], column.to_broadcast([P, P]), ident[:])
             bank_queue.append(number)
-            nc.scalar.copy(
-                out=temp_all_pairs[:, :, PACK * half : PACK * (half + 1)],
-                in_=bank[:].rearrange("p (w n) -> p n w", w=PACK),
-            )
+            nc.scalar.copy(out=temp_all_pairs[:, :, w0 : w0 + PACK], in_=bank[:].rearrange("p (w n) -> p n w", w=PACK))
 
         x_codes = [keep.tile([P, PASSES, BLOCK], U32, name="x_codes%d" % b, align_bytes=64) for b in range(BLOCKS)]
         x_scales = [keep.tile([P, PASSES, BLOCK], U8, name="x_scales%d" % b, align_bytes=64) for b in range(BLOCKS)]
@@ -336,18 +124,17 @@ def tile_router_hidden_tanh_g1_kernel(tc, x, w_hidden, b_hidden, gain, inv_temp,
         y_turned = {}
         y_grouped = {}
         y_codes = {}
-        open_banks = {}
 
         def turn_x(b, c, half, engine):
             if (b, c) not in x_grouped:
                 x_grouped[b, c] = work.tile([P, BLOCK * PACK], BF16, name="x_grouped", bufs=4, align_bytes=64)
             number, bank = take_bank()
-            for jj in range(2):
+            for j in range(HALF // P):
+                pairs = x_pairs[(b * BLOCK + half * HALF) // P + j, c]
                 for u in range(2):
-                    columns = slice(2 * P * u + P * jj, 2 * P * u + P * (jj + 1))
-                    nc.tensor.transpose(bank[:, columns], x_words[4 * b + 2 * half + jj, c][:, u : 2 * P : 2], ident[:])
+                    nc.tensor.transpose(bank[:, HALF * u + P * j : HALF * u + P * (j + 1)], pairs[:, u : 2 * P : 2], ident[:])
             bank_queue.append(number)
-            target = x_grouped[b, c][:].bitcast(F32)[:, BLOCK * half : BLOCK * (half + 1)]
+            target = x_grouped[b, c][:].bitcast(F32)[:, 2 * HALF * half : 2 * HALF * (half + 1)]
             copy_on(engine, target.rearrange("p (n u) -> p n u", u=2), bank[:].rearrange("p (u n) -> p n u", u=2))
 
         def quantize_x(b, c, start, count):
@@ -360,10 +147,9 @@ def tile_router_hidden_tanh_g1_kernel(tc, x, w_hidden, b_hidden, gain, inv_temp,
         def group_w(g, c, half, engine):
             if (g, c) not in w_grouped:
                 w_grouped[g, c] = work.tile([P, K_PASS * PACK], BF16, name="w_grouped", bufs=3, align_bytes=64)
-            target = w_grouped[g, c][:].rearrange("p (t m j) -> p t m j", t=PACK, j=PACK)
-            source = w_raw[g, c][:].rearrange("p j (m t) -> p t m j", t=PACK)
-            part = slice(2 * half, 2 * half + 2) if half < 2 else slice(0, PACK)
-            copy_on(engine, target[:, part], source[:, part])
+            target = w_grouped[g, c][:].rearrange("p (t a i j) -> p t a j i", t=PACK, i=2, j=PACK)
+            source = w_raw[g, c][:].rearrange("p j (a i t) -> p t a j i", t=PACK, i=2)
+            copy_on(engine, target[:, 2 * half : 2 * half + 2], source[:, 2 * half : 2 * half + 2])
 
         def quantize_w(g, c):
             nc.vector.quantize_mx(
@@ -373,12 +159,12 @@ def tile_router_hidden_tanh_g1_kernel(tc, x, w_hidden, b_hidden, gain, inv_temp,
         def mx_pass(unit, t, c, bank):
             g, first, count = unit
             b, start = divmod(first, BLOCK)
-            channels = slice(t * P, (t + 1) * P)
+            columns = slice(t * P, (t + 1) * P)
             tokens = slice(start, start + count)
             nc.tensor.matmul_mx(
                 out=bank[:, 0:count],
-                lhsT=w_codes[g][:, c, channels].bitcast(FP8X4),
-                lhsT_scale=w_scales[g][:, c, channels],
+                lhsT=w_codes[g][:, c, columns].bitcast(FP8X4),
+                lhsT_scale=w_scales[g][:, c, columns],
                 rhs=x_codes[b][:, c, tokens].bitcast(FP8X4),
                 rhs_scale=x_scales[b][:, c, tokens],
                 start=(c == 0),
@@ -415,12 +201,12 @@ def tile_router_hidden_tanh_g1_kernel(tc, x, w_hidden, b_hidden, gain, inv_temp,
         def group_y(unit, half):
             g, first, count = unit
             if unit not in y_grouped:
-                y_grouped[unit] = work.tile([P, BLOCK * PACK], BF16, name="y_grouped", bufs=2, align_bytes=64)
-            tokens = slice(half * count // 2, (half + 1) * count // 2) if half < 2 else slice(0, count)
+                y_grouped[unit] = work.tile([P, BLOCK * PACK], BF16, name="y_grouped", align_bytes=64)
+            tokens = slice(half * count // 2, (half + 1) * count // 2)
             target = y_grouped[unit][:].rearrange("p (n t) -> p n t", t=PACK)[:, tokens, :]
             nc.vector.tensor_copy(
-                out=target.rearrange("p (c i) t -> p c t i", i=2),
-                in_=y_turned[unit][:, :, tokens].rearrange("p t (c i) -> p c t i", i=2),
+                out=target.rearrange("p (a i) t -> p a t i", i=2),
+                in_=y_turned[unit][:, :, tokens].rearrange("p t (a i) -> p a t i", i=2),
             )
 
         def quantize_y(unit):
@@ -438,76 +224,129 @@ def tile_router_hidden_tanh_g1_kernel(tc, x, w_hidden, b_hidden, gain, inv_temp,
 
         def store_scales(g, first, count):
             columns = slice(first // 4, (first + count) // 4)
-            for q in range(4):
+            for q in range(P // QUADRANT):
                 nc.sync.dma_start(
                     out=scales_out[g, 4 * q : 4 * q + 4, columns],
-                    in_=y_scales[g][32 * q : 32 * q + 4, :].bitcast(I32)[:, columns],
+                    in_=y_scales[g][QUADRANT * q : QUADRANT * q + 4, :].bitcast(I32)[:, columns],
                 )
 
-        def turn_y(unit, j, engine):
+        def turn_y(unit, j):
             g, first, count = unit
+            if j >= count // P:
+                return
             number, bank = take_bank()
             for t in range(PACK):
                 nc.tensor.transpose(bank[:, t * P : (t + 1) * P], y_turned[unit][:, t, j * P : (j + 1) * P], ident[:])
             bank_queue.append(number)
             y_rows = work.tile([P, K_PASS], F32, name="y_rows", bufs=6)
-            copy_on(
-                engine,
-                y_rows[:].rearrange("p (m t) -> p m t", t=PACK),
-                bank[:].rearrange("p (t m) -> p m t", t=PACK),
+            nc.scalar.copy(
+                out=y_rows[:].rearrange("p (m t) -> p m t", t=PACK), in_=bank[:].rearrange("p (t m) -> p m t", t=PACK)
             )
             row = first + j * P
             nc.sync.dma_start(out=out_0[row : row + P, g * K_PASS : (g + 1) * K_PASS], in_=y_rows[:])
 
-        def open_pass(unit, t, c):
-            if c == 0:
-                open_banks[unit, t] = take_bank()
-            number, bank = open_banks[unit, t]
-            mx_pass(unit, t, c, bank)
-            if c == PASSES - 1:
-                bank_queue.append(number)
-                activate(unit, t, bank)
-
-        def warm_up(count):
-            number, bank = take_bank()
-            for n in range(count):
-                nc.tensor.matmul_mx(
-                    out=bank[:],
-                    lhsT=w_codes[0][:, 0, 0:P].bitcast(FP8X4),
-                    lhsT_scale=w_scales[0][:, 0, 0:P],
-                    rhs=w_codes[0][:, 0, :].bitcast(FP8X4),
-                    rhs_scale=w_scales[0][:, 0, :],
-                    start=True,
-                    stop=True,
-                )
+        head = UNITS[0]
+        turn_x(0, 0, 0, "scalar")
+        group_w(0, 0, 0, "scalar")
+        quantize_x(0, 0, 0, HALF)
+        group_w(0, 0, 1, "vector")
+        turn_x(0, 1, 0, "scalar")
+        turn_x(0, 2, 0, "scalar")
+        quantize_w(0, 0)
+        open_banks = []
+        for t in range(PACK):
+            open_banks.append(take_bank())
+            mx_pass(head, t, 0, open_banks[t][1])
+        group_w(0, 1, 0, "vector")
+        group_w(0, 1, 1, "vector")
+        quantize_x(0, 1, 0, HALF)
+        quantize_w(0, 1)
+        group_w(0, 2, 0, "scalar")
+        group_w(0, 2, 1, "vector")
+        quantize_x(0, 2, 0, HALF)
+        quantize_w(0, 2)
+        turn_x(0, 0, 1, "scalar")
+        turn_x(0, 1, 1, "scalar")
+        turn_x(0, 2, 1, "vector")
+        quantize_x(0, 0, HALF, HALF)
+        quantize_x(0, 1, HALF, HALF)
+        for t in range(PACK):
+            mx_pass(head, t, 1, open_banks[t][1])
+        for t in range(PACK):
+            number, bank = open_banks[t]
+            mx_pass(head, t, 2, bank)
             bank_queue.append(number)
+            activate(head, t, bank)
+        scale_y(head, 0)
+        quantize_x(0, 2, HALF, HALF)
+        for t in range(1, PACK):
+            scale_y(head, t)
 
-        engines = ("scalar", "vector")
-        for step in PLAN:
-            kind = step[0]
-            if kind == "p":
-                open_pass(UNITS[step[1]], step[2], step[3])
-            elif kind == "m":
-                multiply(UNITS[step[1]], step[2])
-            elif kind == "s":
-                scale_y(UNITS[step[1]], step[2])
-            elif kind == "x":
-                turn_x(step[1], step[2], step[3], engines[step[4]])
-            elif kind == "q":
-                quantize_x(*step[1:])
-            elif kind == "y":
-                turn_y(UNITS[step[1]], step[2], engines[step[3]])
-            elif kind == "g":
-                group_y(UNITS[step[1]], step[2])
-            elif kind == "z":
-                quantize_y(UNITS[step[1]])
-            elif kind == "c":
-                store_codes(UNITS[step[1]])
-            elif kind == "e":
-                store_scales(*step[1:])
-            elif kind == "w":
-                group_w(step[1], step[2], step[3], engines[step[4]])
-            elif kind == "d":
-                warm_up(step[1])
-            elif kind == "v":
-                quantize_w(step[1], step[2])
+        for i in range(1, BLOCKS):
+            unit, before = UNITS[i], UNITS[i - 1]
+            w_pass = i - 2
+            turn_x(i, 0, 0, "scalar")
+            group_y(before, 0)
+            turn_x(i, 0, 1, "scalar")
+            multiply(unit, 0)
+            turn_x(i, 1, 0, "scalar")
+            turn_x(i, 1, 1, "scalar")
+            group_y(before, 1)
+            turn_y(before, 0)
+            multiply(unit, 1)
+            if w_pass >= 0:
+                group_w(1, w_pass, 0, "vector")
+            quantize_y(before)
+            quantize_x(i, 0, 0, BLOCK)
+            turn_x(i, 2, 0, "scalar")
+            if w_pass >= 0:
+                group_w(1, w_pass, 1, "vector")
+            turn_x(i, 2, 1, "scalar")
+            turn_y(before, 1)
+            multiply(unit, 2)
+            scale_y(unit, 0)
+            if w_pass >= 0:
+                quantize_w(1, w_pass)
+            quantize_x(i, 1, 0, BLOCK)
+            turn_y(before, 2)
+            quantize_x(i, 2, 0, BLOCK)
+            turn_y(before, 3)
+            multiply(unit, 3)
+            scale_y(unit, 1)
+            scale_y(unit, 2)
+            store_codes(before)
+            scale_y(unit, 3)
+
+        for i in range(BLOCKS, len(UNITS)):
+            unit, before = UNITS[i], UNITS[i - 1]
+            last_w_pass = i == BLOCKS
+            for t in range(PACK):
+                multiply(unit, t)
+            if last_w_pass:
+                group_w(1, PASSES - 1, 0, "vector")
+                group_w(1, PASSES - 1, 1, "vector")
+            group_y(before, 0)
+            if last_w_pass:
+                quantize_w(1, PASSES - 1)
+            scale_y(unit, 0)
+            group_y(before, 1)
+            for t in range(1, PACK):
+                scale_y(unit, t)
+            for j in range(BLOCK // P):
+                turn_y(before, j)
+            quantize_y(before)
+            store_codes(before)
+            g, first, count = before
+            if g == 0 and first + count == TOKENS:
+                store_scales(0, 0, TOKENS)
+            if g == 1 and first + count == TOKENS - BLOCK:
+                store_scales(1, 0, TOKENS - BLOCK)
+
+        last = UNITS[-1]
+        group_y(last, 0)
+        group_y(last, 1)
+        turn_y(last, 0)
+        quantize_y(last)
+        turn_y(last, 1)
+        store_codes(last)
+        store_scales(1, TOKENS - BLOCK, BLOCK)

from contextlib import ExitStack

import concourse.mybir as mybir
from concourse.masks import make_identity

TOKENS, MODEL, HIDDEN = 2048, 1536, 1024
FLOPS = 2 * TOKENS * MODEL * HIDDEN

F32 = mybir.dt.float32
BF16 = mybir.dt.bfloat16
U32 = mybir.dt.uint32
I32 = mybir.dt.int32
U8 = mybir.dt.uint8
FP8X4 = mybir.dt.float8_e4m3fn_x4
TANH = mybir.ActivationFunctionType.Tanh
MULT = mybir.AluOpType.mult

P = 128
PACK = 4
K_PASS = P * PACK
PASSES = MODEL // K_PASS
GROUPS = HIDDEN // K_PASS
BLOCK = 512
HALF = BLOCK // 2
BLOCKS = TOKENS // BLOCK
BANKS = 8
QUADRANT = 32

UNITS = (
    [(0, 0, HALF), (0, HALF, HALF)]
    + [(0, b * BLOCK, BLOCK) for b in range(1, BLOCKS)]
    + [(1, b * BLOCK, BLOCK) for b in range(BLOCKS - 1)]
    + [(1, TOKENS - BLOCK, HALF), (1, TOKENS - HALF, HALF)]
)


def tile_router_hidden_tanh_g1_kernel(tc, x, w_hidden, b_hidden, gain, inv_temp, out_0, out_1, out_2):
    nc = tc.nc
    words_out = out_1.rearrange("g p m t -> g p (m t)").bitcast(I32)
    scales_out = out_2.bitcast(I32)

    with ExitStack() as ctx:
        keep = ctx.enter_context(tc.tile_pool(name="keep", bufs=1))
        work = ctx.enter_context(tc.tile_pool(name="work", bufs=2))
        psum = ctx.enter_context(tc.psum_pool(name="psum", bufs=1))
        ctx.enter_context(tc.manual_schedule())

        bank_queue = list(range(BANKS))

        def take_bank():
            number = bank_queue[0]
            bank_queue.remove(number)
            bank = psum.tile([P, BLOCK], F32, name="bank%d" % number)
            return number, bank

        def copy_on(engine, out, in_):
            if engine == "scalar":
                nc.scalar.copy(out=out, in_=in_)
            else:
                nc.vector.tensor_copy(out=out, in_=in_)

        temps_a_row = TOKENS // P
        temp_rows = keep.tile([P, temps_a_row], BF16)
        bias = keep.tile([P, GROUPS, PACK], BF16)
        gains = keep.tile([P, GROUPS, PACK], BF16)
        nc.scalar.dma_start(out=temp_rows[:], in_=inv_temp.rearrange("(n j) -> n j", n=P))
        nc.scalar.dma_start(out=bias[:], in_=b_hidden.rearrange("(g p t) -> p g t", p=P, t=PACK))
        nc.scalar.dma_start(out=gains[:], in_=gain.rearrange("(g p t) -> p g t", p=P, t=PACK))

        ident = keep.tile([P, P], F32)
        make_identity(nc, ident[:])
        warm = keep.tile([P, 2], F32)
        nc.vector.memset(warm[:, 0:1], 0.0)
        nc.scalar.activation(out=warm[:, 1:2], in_=warm[:, 0:1], func=TANH)

        x_pairs = {}
        w_raw = {}

        def load_x(first, count):
            raw = keep.tile([P, count // P, MODEL], BF16, name="x_raw%d" % first)
            nc.sync.dma_start(out=raw[:], in_=x[first : first + count, :].rearrange("(j p) k -> p j k", p=P))
            for j in range(count // P):
                for c in range(PASSES):
                    x_pairs[first // P + j, c] = raw[:, j, c * K_PASS : (c + 1) * K_PASS].bitcast(F32)

        def load_w(g, c):
            raw = keep.tile([P, PACK, K_PASS], BF16, name="w_raw%d_%d" % (g, c))
            rows = w_hidden[c * K_PASS : (c + 1) * K_PASS, g * K_PASS : (g + 1) * K_PASS]
            nc.sync.dma_start(out=raw[:], in_=rows.rearrange("(p j) n -> p j n", j=PACK))
            w_raw[g, c] = raw

        load_x(0, HALF)
        load_w(0, 0)
        load_w(0, 1)
        load_x(HALF, HALF)
        load_w(0, 2)
        load_x(BLOCK, HALF)
        load_x(BLOCK + HALF, HALF)
        load_x(2 * BLOCK, BLOCK)
        load_w(1, 0)
        load_x(3 * BLOCK, BLOCK)
        load_w(1, 1)
        load_w(1, 2)

        temp_all = keep.tile([P, TOKENS], BF16)
        temp_pairs = temp_rows[:].bitcast(F32)
        temp_all_pairs = temp_all[:].bitcast(F32).rearrange("p (n w) -> p n w", n=P)
        for w0 in range(0, temps_a_row // 2, PACK):
            number, bank = take_bank()
            for w in range(PACK):
                column = temp_pairs[:, w0 + w : w0 + w + 1]
                nc.tensor.transpose(bank[:, w * P : (w + 1) * P], column.to_broadcast([P, P]), ident[:])
            bank_queue.append(number)
            nc.scalar.copy(out=temp_all_pairs[:, :, w0 : w0 + PACK], in_=bank[:].rearrange("p (w n) -> p n w", w=PACK))

        x_codes = [keep.tile([P, PASSES, BLOCK], U32, name="x_codes%d" % b, align_bytes=64) for b in range(BLOCKS)]
        x_scales = [keep.tile([P, PASSES, BLOCK], U8, name="x_scales%d" % b, align_bytes=64) for b in range(BLOCKS)]
        w_codes = [keep.tile([P, PASSES, K_PASS], U32, name="w_codes%d" % g, align_bytes=64) for g in range(GROUPS)]
        w_scales = [keep.tile([P, PASSES, K_PASS], U8, name="w_scales%d" % g, align_bytes=64) for g in range(GROUPS)]
        y_scales = [keep.tile([P, TOKENS], U8, name="y_scales%d" % g, align_bytes=64) for g in range(GROUPS)]
        x_grouped = {}
        w_grouped = {}
        hidden = {}
        y_turned = {}
        y_grouped = {}
        y_codes = {}

        def turn_x(b, c, half, engine):
            if (b, c) not in x_grouped:
                x_grouped[b, c] = work.tile([P, BLOCK * PACK], BF16, name="x_grouped", bufs=4, align_bytes=64)
            number, bank = take_bank()
            for j in range(HALF // P):
                pairs = x_pairs[(b * BLOCK + half * HALF) // P + j, c]
                for u in range(2):
                    nc.tensor.transpose(bank[:, HALF * u + P * j : HALF * u + P * (j + 1)], pairs[:, u : 2 * P : 2], ident[:])
            bank_queue.append(number)
            target = x_grouped[b, c][:].bitcast(F32)[:, 2 * HALF * half : 2 * HALF * (half + 1)]
            copy_on(engine, target.rearrange("p (n u) -> p n u", u=2), bank[:].rearrange("p (u n) -> p n u", u=2))

        def quantize_x(b, c, start, count):
            nc.vector.quantize_mx(
                out=x_codes[b][:, c, start : start + count].bitcast(FP8X4),
                scales=x_scales[b][:, c, start : start + count],
                in_=x_grouped[b, c][:, start * PACK : (start + count) * PACK],
            )

        def group_w(g, c, half, engine):
            if (g, c) not in w_grouped:
                w_grouped[g, c] = work.tile([P, K_PASS * PACK], BF16, name="w_grouped", bufs=3, align_bytes=64)
            target = w_grouped[g, c][:].rearrange("p (t a i j) -> p t a j i", t=PACK, i=2, j=PACK)
            source = w_raw[g, c][:].rearrange("p j (a i t) -> p t a j i", t=PACK, i=2)
            copy_on(engine, target[:, 2 * half : 2 * half + 2], source[:, 2 * half : 2 * half + 2])

        def quantize_w(g, c):
            nc.vector.quantize_mx(
                out=w_codes[g][:, c, :].bitcast(FP8X4), scales=w_scales[g][:, c, :], in_=w_grouped[g, c][:]
            )

        def mx_pass(unit, t, c, bank):
            g, first, count = unit
            b, start = divmod(first, BLOCK)
            columns = slice(t * P, (t + 1) * P)
            tokens = slice(start, start + count)
            nc.tensor.matmul_mx(
                out=bank[:, 0:count],
                lhsT=w_codes[g][:, c, columns].bitcast(FP8X4),
                lhsT_scale=w_scales[g][:, c, columns],
                rhs=x_codes[b][:, c, tokens].bitcast(FP8X4),
                rhs_scale=x_scales[b][:, c, tokens],
                start=(c == 0),
                stop=(c == PASSES - 1),
            )

        def activate(unit, t, bank):
            g, first, count = unit
            hidden[unit, t] = work.tile([P, BLOCK], F32, name="hidden", bufs=4)
            nc.scalar.activation(
                out=hidden[unit, t][:, 0:count], in_=bank[:, 0:count], func=TANH, bias=bias[:, g, t : t + 1]
            )

        def multiply(unit, t):
            number, bank = take_bank()
            for c in range(PASSES):
                mx_pass(unit, t, c, bank)
            bank_queue.append(number)
            activate(unit, t, bank)

        def scale_y(unit, t):
            g, first, count = unit
            if unit not in y_turned:
                y_turned[unit] = work.tile([P, PACK, BLOCK], F32, name="y_turned", bufs=3)
            nc.vector.scalar_tensor_tensor(
                out=y_turned[unit][:, t, 0:count],
                in0=temp_all[:, first : first + count],
                scalar=gains[:, g, t : t + 1],
                in1=hidden[unit, t][:, 0:count],
                op0=MULT,
                op1=MULT,
            )

        def group_y(unit, half):
            g, first, count = unit
            if unit not in y_grouped:
                y_grouped[unit] = work.tile([P, BLOCK * PACK], BF16, name="y_grouped", align_bytes=64)
            tokens = slice(half * count // 2, (half + 1) * count // 2)
            target = y_grouped[unit][:].rearrange("p (n t) -> p n t", t=PACK)[:, tokens, :]
            nc.vector.tensor_copy(
                out=target.rearrange("p (a i) t -> p a t i", i=2),
                in_=y_turned[unit][:, :, tokens].rearrange("p t (a i) -> p a t i", i=2),
            )

        def quantize_y(unit):
            g, first, count = unit
            y_codes[unit] = work.tile([P, BLOCK], U32, name="y_codes", bufs=3, align_bytes=64)
            nc.vector.quantize_mx(
                out=y_codes[unit][:, 0:count].bitcast(FP8X4),
                scales=y_scales[g][:, first : first + count],
                in_=y_grouped[unit][:, 0 : count * PACK],
            )

        def store_codes(unit):
            g, first, count = unit
            nc.sync.dma_start(out=words_out[g, :, first : first + count], in_=y_codes[unit][:, 0:count].bitcast(I32))

        def store_scales(g, first, count):
            columns = slice(first // 4, (first + count) // 4)
            for q in range(P // QUADRANT):
                nc.sync.dma_start(
                    out=scales_out[g, 4 * q : 4 * q + 4, columns],
                    in_=y_scales[g][QUADRANT * q : QUADRANT * q + 4, :].bitcast(I32)[:, columns],
                )

        def turn_y(unit, j):
            g, first, count = unit
            if j >= count // P:
                return
            number, bank = take_bank()
            for t in range(PACK):
                nc.tensor.transpose(bank[:, t * P : (t + 1) * P], y_turned[unit][:, t, j * P : (j + 1) * P], ident[:])
            bank_queue.append(number)
            y_rows = work.tile([P, K_PASS], F32, name="y_rows", bufs=6)
            nc.scalar.copy(
                out=y_rows[:].rearrange("p (m t) -> p m t", t=PACK), in_=bank[:].rearrange("p (t m) -> p m t", t=PACK)
            )
            row = first + j * P
            nc.sync.dma_start(out=out_0[row : row + P, g * K_PASS : (g + 1) * K_PASS], in_=y_rows[:])

        head = UNITS[0]
        turn_x(0, 0, 0, "scalar")
        group_w(0, 0, 0, "scalar")
        quantize_x(0, 0, 0, HALF)
        group_w(0, 0, 1, "vector")
        turn_x(0, 1, 0, "scalar")
        turn_x(0, 2, 0, "scalar")
        quantize_w(0, 0)
        open_banks = []
        for t in range(PACK):
            open_banks.append(take_bank())
            mx_pass(head, t, 0, open_banks[t][1])
        group_w(0, 1, 0, "vector")
        group_w(0, 1, 1, "vector")
        quantize_x(0, 1, 0, HALF)
        quantize_w(0, 1)
        group_w(0, 2, 0, "scalar")
        group_w(0, 2, 1, "vector")
        quantize_x(0, 2, 0, HALF)
        quantize_w(0, 2)
        turn_x(0, 0, 1, "scalar")
        turn_x(0, 1, 1, "scalar")
        turn_x(0, 2, 1, "vector")
        quantize_x(0, 0, HALF, HALF)
        quantize_x(0, 1, HALF, HALF)
        for t in range(PACK):
            mx_pass(head, t, 1, open_banks[t][1])
        for t in range(PACK):
            number, bank = open_banks[t]
            mx_pass(head, t, 2, bank)
            bank_queue.append(number)
            activate(head, t, bank)
        scale_y(head, 0)
        quantize_x(0, 2, HALF, HALF)
        for t in range(1, PACK):
            scale_y(head, t)

        for i in range(1, BLOCKS):
            unit, before = UNITS[i], UNITS[i - 1]
            w_pass = i - 2
            turn_x(i, 0, 0, "scalar")
            group_y(before, 0)
            turn_x(i, 0, 1, "scalar")
            multiply(unit, 0)
            turn_x(i, 1, 0, "scalar")
            turn_x(i, 1, 1, "scalar")
            group_y(before, 1)
            turn_y(before, 0)
            multiply(unit, 1)
            if w_pass >= 0:
                group_w(1, w_pass, 0, "vector")
            quantize_y(before)
            quantize_x(i, 0, 0, BLOCK)
            turn_x(i, 2, 0, "scalar")
            if w_pass >= 0:
                group_w(1, w_pass, 1, "vector")
            turn_x(i, 2, 1, "scalar")
            turn_y(before, 1)
            multiply(unit, 2)
            scale_y(unit, 0)
            if w_pass >= 0:
                quantize_w(1, w_pass)
            quantize_x(i, 1, 0, BLOCK)
            turn_y(before, 2)
            quantize_x(i, 2, 0, BLOCK)
            turn_y(before, 3)
            multiply(unit, 3)
            scale_y(unit, 1)
            scale_y(unit, 2)
            store_codes(before)
            scale_y(unit, 3)

        for i in range(BLOCKS, len(UNITS)):
            unit, before = UNITS[i], UNITS[i - 1]
            last_w_pass = i == BLOCKS
            for t in range(PACK):
                multiply(unit, t)
            if last_w_pass:
                group_w(1, PASSES - 1, 0, "vector")
                group_w(1, PASSES - 1, 1, "vector")
            group_y(before, 0)
            if last_w_pass:
                quantize_w(1, PASSES - 1)
            scale_y(unit, 0)
            group_y(before, 1)
            for t in range(1, PACK):
                scale_y(unit, t)
            for j in range(BLOCK // P):
                turn_y(before, j)
            quantize_y(before)
            store_codes(before)
            g, first, count = before
            if g == 0 and first + count == TOKENS:
                store_scales(0, 0, TOKENS)
            if g == 1 and first + count == TOKENS - BLOCK:
                store_scales(1, 0, TOKENS - BLOCK)

        last = UNITS[-1]
        group_y(last, 0)
        group_y(last, 1)
        turn_y(last, 0)
        quantize_y(last)
        turn_y(last, 1)
        store_codes(last)
        store_scales(1, TOKENS - BLOCK, BLOCK)
